import numpy as np, ml_dtypes
CORES = [89,94,345,350]
N = 4
TOK, K, FT = 32, 3, 2
ROUTE = [[[0,1,3],[0,1,3],[0,2,3],[0,1,2],[1,2,3],[1,2,3],[0,1,3],[1,2,3],[0,1,2],[0,2,3],[1,2,3],[0,1,3],[0,2,3],[0,1,2],[1,2,3],[0,1,2],[0,1,2],[0,2,3],[0,1,2],[0,1,3],[0,1,3],[0,1,3],[1,2,3],[1,2,3],[0,1,3],[0,2,3],[0,1,3],[0,2,3],[1,2,3],[0,1,3],[0,1,2],[0,1,3]],[[1,2,3],[0,1,2],[0,2,3],[0,1,2],[0,1,3],[0,1,3],[0,1,3],[0,1,3],[0,1,3],[0,1,3],[1,2,3],[0,1,3],[0,1,2],[0,1,3],[1,2,3],[0,1,2],[1,2,3],[0,2,3],[1,2,3],[0,2,3],[0,1,3],[0,2,3],[1,2,3],[0,1,3],[0,1,3],[0,2,3],[0,1,3],[0,1,2],[0,1,3],[1,2,3],[0,1,2],[0,1,3]],[[1,2,3],[0,1,2],[0,1,3],[1,2,3],[0,1,2],[1,2,3],[0,1,3],[1,2,3],[0,1,2],[0,2,3],[0,1,2],[0,1,3],[0,1,2],[0,1,3],[0,1,3],[0,2,3],[1,2,3],[0,1,3],[1,2,3],[1,2,3],[0,2,3],[1,2,3],[0,1,3],[1,2,3],[0,2,3],[0,2,3],[1,2,3],[1,2,3],[0,1,2],[1,2,3],[1,2,3],[0,2,3]],[[0,2,3],[0,1,3],[0,2,3],[0,2,3],[0,1,3],[1,2,3],[1,2,3],[0,2,3],[1,2,3],[0,1,2],[0,2,3],[1,2,3],[0,1,3],[0,2,3],[0,1,3],[0,1,2],[0,1,3],[1,2,3],[1,2,3],[0,1,2],[1,2,3],[0,1,2],[0,2,3],[1,2,3],[1,2,3],[0,1,2],[1,2,3],[0,2,3],[0,2,3],[0,1,3],[1,2,3],[1,2,3]]]
def setup_inputs(rng):
    return {"x": rng.standard_normal((N, 128, TOK), dtype=np.float32).astype(ml_dtypes.bfloat16), "gate": (0.5 * rng.integers(1, 4, size=(N, K, TOK)) * (2 * rng.integers(0, 2, size=(N, K, TOK)) - 1)).astype(np.float32).astype(ml_dtypes.bfloat16), "w1": (rng.standard_normal((N, 128, FT * 128), dtype=np.float32) / 8).astype(ml_dtypes.bfloat16), "w2": (rng.standard_normal((N, 128, FT * 128), dtype=np.float32) / 8).astype(ml_dtypes.bfloat16)}
def setup_inputs_big(rng):
    d = setup_inputs(rng)
    for k in ("x", "gate", "w1", "w2"): d[k] = (d[k].astype(np.float32) * 1024.0).astype(d[k].dtype)
    return d
def setup_inputs_small(rng):
    d = setup_inputs(rng)
    for k in ("x", "gate", "w1", "w2"): d[k] = (d[k].astype(np.float32) * (1 / 1024.0)).astype(d[k].dtype)
    return d
def reference(x, gate, w1, w2):
    X, GATE, W1, W2 = x.astype(np.float64), gate.astype(np.float64), w1.astype(np.float64), w2.astype(np.float64)
    y = np.zeros((N, 128, TOK))
    for r in range(N):
        for t in range(TOK):
            for i, e in enumerate(ROUTE[r][t]):
                hid = np.maximum(W1[e].T @ X[r][:, t], 0.0)
                y[r][:, t] += GATE[r][i, t] * sum(W2[e][:, 128 * f:128 * f + 128].T @ hid[128 * f:128 * f + 128] for f in range(FT))
    return {"y": y.astype(ml_dtypes.bfloat16)}

@@ -1,0 +1,204 @@
+from concourse.bass import DstId, RemoteDMATransfer
+from concourse.mybir import AluOpType
+
+P = 128
+TOK, K, FT = 32, 3, 2
+NSIM = 512
+NT = 2 * TOK
+WS = 2 * FT * P
+GP = 32
+
+SCRATCH = {
+    "xl": ("sbuf", [P, 2 * NT], "bfloat16"),
+    "wb": ("sbuf", [P, 2 * WS], "bfloat16"),
+    "ones": ("sbuf", [P, P], "bfloat16"),
+    "zero": ("sbuf", [P, FT * NT], "float32"),
+    "mask": ("sbuf", [P, 2 * NT], "bfloat16"),
+    "pm": ("sbuf", [P, 2 * NT], "bfloat16"),
+    "gs": ("sbuf", [P, 2 * NT], "float32"),
+    "h": ("sbuf", [P, 2 * FT * NT], "bfloat16"),
+    "res": ("sbuf", [P, 2 * NT], "bfloat16"),
+    "sl": ("sbuf", [P, TOK], "bfloat16"),
+    "al": ("sbuf", [P, TOK], "bfloat16"),
+    "acc": ("sbuf", [P, TOK], "bfloat16"),
+    "yb": ("sbuf", [P, TOK], "bfloat16"),
+    "z0": ("psum", [P, 512], "float32"),
+    "z1": ("psum", [P, 512], "float32"),
+    "o0": ("psum", [P, 512], "float32"),
+    "o1": ("psum", [P, 512], "float32"),
+    "gp": ("psum", [P, 512], "float32"),
+}
+SEMAPHORES = ["ms", "xld", "xa", "w0", "w1", "c0", "c", "pm", "gp", "gs", "z0", "z1", "h0", "h1", "o0", "o1",
+              "r", "sa", "fa", "acc", "ybs", "yd", "loc"]
+
+
+def _bits(m):
+    return [b for b in range(m.bit_length()) if (m >> b) & 1]
+
+
+def _mk(bits):
+    return sum(1 << b for b in bits)
+
+
+def _gc(p):
+    return (0, TOK) if p == 0 else (2 * NT - TOK, 2 * NT)
+
+
+def _site(g, T, route, TR, ER, xwaits, wwaits):
+    V, TE, sem = g.vector, g.tensor, T.sem
+    ne = len(ER)
+    V.memset(T.mask[:, 0:ne * NT], 0.0).then_inc(sem.c0, 1)
+    V.memset(T.zero[:, :], 0.0).then_inc(sem.c, 1)
+    V.memset(T.ones[:, :], 1.0).then_inc(sem.c, 1)
+    nc = 2
+    V.wait_ge(sem.c0, 1)
+    for i in range(K):
+        flags = [route[r][t][i] == e for e in ER for r in TR for t in range(TOK)] + [False]
+        a = None
+        for c, fl in enumerate(flags):
+            if fl and a is None:
+                a = c
+            if not fl and a is not None:
+                V.memset(T.mask[GP * i:GP * (i + 1), a:c], 1.0).then_inc(sem.c, 1)
+                nc += 1
+                a = None
+    V.wait_ge(sem.c, nc)
+    TE.wait_ge(sem.c, nc)
+    for s, n in xwaits:
+        V.wait_ge(s, n)
+        TE.wait_ge(s, n)
+    for e in range(ne):
+        for p in range(len(TR)):
+            b = e * NT + p * TOK
+            lo, hi = _gc(p)
+            V.tensor_tensor(out=T.pm[:, b:b + TOK], in0=T.xl[:, lo:hi], in1=T.mask[:, b:b + TOK],
+                            op=AluOpType.mult).then_inc(sem.pm, 1)
+    TE.wait_ge(sem.pm, ne * len(TR))
+    TE.matmul(out=T.gp[:, 0:ne * NT], lhsT=T.ones[:, :], rhs=T.pm[:, 0:ne * NT], start=True, stop=True).then_inc(sem.gp, 1)
+    V.wait_ge(sem.gp, 1)
+    V.tensor_copy(out=T.gs[:, 0:ne * NT], in_=T.gp[:, 0:ne * NT]).then_inc(sem.gs, 1)
+    for e in range(ne):
+        TE.wait_ge(wwaits[e][0], wwaits[e][1])
+        for f in range(FT):
+            TE.matmul(out=T["z%d" % e][:, f * NT:(f + 1) * NT], lhsT=T.wb[:, e * WS + f * P:e * WS + (f + 1) * P],
+                      rhs=T.xl[:, TOK:TOK + NT], start=True, stop=True).then_inc(sem["z%d" % e], 1)
+    for e in range(ne):
+        V.wait_ge(sem["z%d" % e], FT)
+        V.tensor_tensor(out=T.h[:, e * FT * NT:(e + 1) * FT * NT], in0=T["z%d" % e][:, 0:FT * NT], in1=T.zero[:, :],
+                        op=AluOpType.max).then_inc(sem["h%d" % e], 1)
+    for e in range(ne):
+        TE.wait_ge(sem["h%d" % e], 1)
+        for f in range(FT):
+            w = e * WS + FT * P + f * P
+            TE.matmul(out=T["o%d" % e][:, 0:NT], lhsT=T.wb[:, w:w + P],
+                      rhs=T.h[:, (e * FT + f) * NT:(e * FT + f + 1) * NT],
+                      start=(f == 0), stop=(f == FT - 1)).then_inc(sem["o%d" % e], 1)
+    V.wait_ge(sem.gs, 1)
+    for e in range(ne):
+        V.wait_ge(sem["o%d" % e], FT)
+        V.tensor_tensor(out=T.res[:, e * NT:(e + 1) * NT], in0=T["o%d" % e][:, 0:NT], in1=T.gs[:, e * NT:(e + 1) * NT],
+                        op=AluOpType.mult).then_inc(sem.r, 1)
+
+
+def rank_program(g, core, T, topo):
+    cores = list(T.cores)
+    route = T.tables["ROUTE"]
+    sem = T.sem
+    hosts = []
+    for c in cores:
+        if topo.host(c) not in hosts:
+            hosts.append(topo.host(c))
+    sides = [[r for r in range(len(cores)) if topo.host(cores[r]) == h] for h in hosts]
+    helpers = []
+    for s, side in enumerate(sides):
+        first = cores[side[0]]
+        pick = None
+        for w in range(NSIM):
+            if pick is not None or w in cores or topo.host(w) in hosts:
+                continue
+            if topo.chip(w) != topo.chip(first) or topo.die(w) != topo.die(first):
+                continue
+            if topo.rack(topo.host(w)) != topo.rack(topo.host(first)):
+                continue
+            if all(topo.may_write(c, w) for c in cores) and all(topo.may_write(w, cores[r]) for r in side):
+                pick = w
+        helpers.append(pick)
+
+    rank = T.rank_of(core)
+    if rank is None:
+        if core not in helpers:
+            return
+        s = helpers.index(core)
+        side, far = sides[s], sides[1 - s]
+        nx = sum(len(_bits(topo.mask(cores[r], core))) for r in side)
+        ww = [(sem["w%d" % e], len(_bits(topo.mask(cores[far[e]], core)))) for e in range(len(far))]
+        _site(g, T, route, side, far, [(sem.xa, nx)], ww)
+        g.wait_ge(sem.r, len(far))
+        trs, nloc = [], 0
+        for p, r in enumerate(side):
+            bits = _bits(topo.mask(core, cores[r]))
+            n = len(bits) // len(side)
+            rid, pid = topo.addr(cores[r], core)
+            trs.append(RemoteDMATransfer(dst_ids=[DstId(rid=rid, pnc=pid)], dma_engine_mask=_mk(bits[p * n:(p + 1) * n]),
+                                         remote_sem=sem.fa,
+                                         srcs=[T.res[:, e * NT + p * TOK:e * NT + (p + 1) * TOK] for e in range(len(far))],
+                                         dsts=[T.al[:, :]], alu_op=1))
+            nloc += n
+        g.remote_dma_fused(trs, local_sem=sem.loc)
+        g.wait_ge(sem.loc, nloc)
+        return
+
+    s = [rank in side for side in sides].index(True)
+    side = sides[s]
+    p = side.index(rank)
+    sib = cores[side[1 - p]]
+    hx, hw = helpers[s], helpers[1 - s]
+    lo, hi = _gc(p)
+    V = g.vector
+    V.memset(T.xl[:, lo:hi], 0.0).then_inc(sem.ms, 1)
+    g.sync.dma_start(T.xl[:, TOK + p * TOK:TOK + (p + 1) * TOK], T.x[:, :]).then_inc(sem.xld, 16)
+    g.scalar.wait_ge(sem.ms, 1)
+    g.scalar.dma_start(T.xl[0:GP * (K - 1) + 1:GP, lo:hi], T.gate[:, :]).then_inc(sem.xld, 16)
+    g.sync.dma_start(T.wb[:, 0:FT * P], T.w1[:, :]).then_inc(sem.w0, 16)
+    g.scalar.dma_start(T.wb[:, FT * P:WS], T.w2[:, :]).then_inc(sem.w0, 16)
+
+    off = _bits(topo.mask(core, hx))
+    offw = _bits(topo.mask(core, hw))
+    on = [b for b in _bits(topo.mask(core, sib)) if b not in off and b not in offw]
+    nloc = 0
+    g.wait_ge(sem.ms, 1)
+    g.wait_ge(sem.xld, 32)
+    rid, pid = topo.addr(hx, core)
+    g.remote_dma(out_ap=T.xl[:, p * NT:(p + 1) * NT], in_ap=T.xl[:, p * NT:(p + 1) * NT], remote_sem=sem.xa,
+                 local_sem=sem.loc, pid=pid, routing_id=rid, dma_engine_mask=_mk(off))
+    nloc += len(off)
+    g.wait_ge(sem.w0, 32)
+    rid, pid = topo.addr(hw, core)
+    g.remote_dma(out_ap=T.wb[:, p * WS:(p + 1) * WS], in_ap=T.wb[:, 0:WS], remote_sem=sem["w%d" % p],
+                 local_sem=sem.loc, pid=pid, routing_id=rid, dma_engine_mask=_mk(offw))
+    nloc += len(offw)
+    rid, pid = topo.addr(sib, core)
+    g.remote_dma(out_ap=T.xl[:, p * NT:(p + 1) * NT], in_ap=T.xl[:, p * NT:(p + 1) * NT], remote_sem=sem.xa,
+                 local_sem=sem.loc, pid=pid, routing_id=rid, dma_engine_mask=_mk(on))
+    nloc += len(on)
+
+    V.wait_ge(sem.ms, 1)
+    _site(g, T, route, side, [rank], [(sem.xld, 32), (sem.xa, len(on))], [(sem.w0, 32)])
+
+    g.wait_ge(sem.r, 1)
+    q = 1 - p
+    g.remote_dma(out_ap=T.sl[:, :], in_ap=T.res[:, q * TOK:(q + 1) * TOK], remote_sem=sem.sa,
+                 local_sem=sem.loc, pid=pid, routing_id=rid, dma_engine_mask=_mk(on))
+    nloc += len(on)
+    g.wait_ge(sem.loc, nloc)
+
+    V.wait_ge(sem.r, 1)
+    V.wait_ge(sem.sa, len(on))
+    V.tensor_tensor(out=T.acc[:, :], in0=T.res[:, p * TOK:(p + 1) * TOK], in1=T.sl[:, :],
+                    op=AluOpType.add).then_inc(sem.acc, 1)
+    V.wait_ge(sem.acc, 1)
+    V.wait_ge(sem.fa, len(_bits(topo.mask(hx, core))) // len(side))
+    V.tensor_tensor(out=T.yb[:, :], in0=T.acc[:, :], in1=T.al[:, :], op=AluOpType.add).then_inc(sem.ybs, 1)
+    g.sync.wait_ge(sem.ybs, 1)
+    g.sync.dma_start(T.y[:, :], T.yb[:, :]).then_inc(sem.yd, 16)
+    g.sync.wait_ge(sem.yd, 16)

@@ -7,6 +7,7 @@ NSIM = 512
 NT = 2 * TOK
 WS = 2 * FT * P
 GP = 32
+TOKEN_RACK = False
 
 SCRATCH = {
     "xl": ("sbuf", [P, 2 * NT], "bfloat16"),
@@ -112,13 +113,14 @@ def rank_program(g, core, T, topo):
     helpers = []
     for s, side in enumerate(sides):
         first = cores[side[0]]
+        near = first if TOKEN_RACK else cores[sides[1 - s][0]]
         pick = None
         for w in range(NSIM):
             if pick is not None or w in cores or topo.host(w) in hosts:
                 continue
             if topo.chip(w) != topo.chip(first) or topo.die(w) != topo.die(first):
                 continue
-            if topo.rack(topo.host(w)) != topo.rack(topo.host(first)):
+            if topo.rack(topo.host(w)) != topo.rack(topo.host(near)):
                 continue
             if all(topo.may_write(c, w) for c in cores) and all(topo.may_write(w, cores[r]) for r in side):
                 pick = w

@@ -1,5 +1,5 @@
 from concourse.bass import DstId, RemoteDMATransfer
-from concourse.mybir import AluOpType
+from concourse.mybir import AluOpType, ActivationFunctionType
 
 P = 128
 TOK, K, FT = 32, 3, 2
@@ -7,21 +7,24 @@ NSIM = 512
 NT = 2 * TOK
 WS = 2 * FT * P
 GP = 32
-TOKEN_RACK = False
 
 SCRATCH = {
     "xl": ("sbuf", [P, 2 * NT], "bfloat16"),
     "wb": ("sbuf", [P, 2 * WS], "bfloat16"),
-    "ones": ("sbuf", [P, P], "bfloat16"),
+    "sel": ("sbuf", [P, K * P], "bfloat16"),
     "zero": ("sbuf", [P, FT * NT], "float32"),
-    "mask": ("sbuf", [P, 2 * NT], "bfloat16"),
+    "on": ("sbuf", [P, TOK], "bfloat16"),
+    "tb": ("sbuf", [P, NT], "bfloat16"),
     "pm": ("sbuf", [P, 2 * NT], "bfloat16"),
     "gs": ("sbuf", [P, 2 * NT], "float32"),
+    "gb": ("sbuf", [P, TOK], "bfloat16"),
     "h": ("sbuf", [P, 2 * FT * NT], "bfloat16"),
     "res": ("sbuf", [P, 2 * NT], "bfloat16"),
     "sl": ("sbuf", [P, TOK], "bfloat16"),
     "al": ("sbuf", [P, TOK], "bfloat16"),
-    "acc": ("sbuf", [P, TOK], "bfloat16"),
+    "a0": ("sbuf", [P, TOK], "float32"),
+    "a1": ("sbuf", [P, TOK], "float32"),
+    "a2": ("sbuf", [P, TOK], "bfloat16"),
     "yb": ("sbuf", [P, TOK], "bfloat16"),
     "z0": ("psum", [P, 512], "float32"),
     "z1": ("psum", [P, 512], "float32"),
@@ -29,8 +32,8 @@ SCRATCH = {
     "o1": ("psum", [P, 512], "float32"),
     "gp": ("psum", [P, 512], "float32"),
 }
-SEMAPHORES = ["ms", "xld", "xa", "w0", "w1", "c0", "c", "pm", "gp", "gs", "z0", "z1", "h0", "h1", "o0", "o1",
-              "r", "sa", "fa", "acc", "ybs", "yd", "loc"]
+SEMAPHORES = ["ms", "xld", "xa", "w0", "w1", "c0", "c1", "t0", "t1", "u0", "u1", "se", "zs", "ta", "pm", "gp", "gs",
+              "z0", "z1", "h0", "h1", "o0", "o1", "r", "sa", "fa", "acc", "ybs", "yd", "loc"]
 
 
 def _bits(m):
@@ -45,48 +48,110 @@ def _gc(p):
     return (0, TOK) if p == 0 else (2 * NT - TOK, 2 * NT)
 
 
-def _site(g, T, route, TR, ER, xwaits, wwaits):
-    V, TE, sem = g.vector, g.tensor, T.sem
-    ne = len(ER)
-    V.memset(T.mask[:, 0:ne * NT], 0.0).then_inc(sem.c0, 1)
-    V.memset(T.zero[:, :], 0.0).then_inc(sem.c, 1)
-    V.memset(T.ones[:, :], 1.0).then_inc(sem.c, 1)
-    nc = 2
-    V.wait_ge(sem.c0, 1)
+def _consts(g, T):
+    V, sem = g.vector, T.sem
+    V.memset(T.sel[:, :], 0.0).then_inc(sem.c1, 1)
+    V.memset(T.zero[:, :], 0.0).then_inc(sem.zs, 1)
+    V.wait_ge(sem.c1, 1)
+    V.wait_ge(sem.zs, 1)
     for i in range(K):
-        flags = [route[r][t][i] == e for e in ER for r in TR for t in range(TOK)] + [False]
-        a = None
-        for c, fl in enumerate(flags):
-            if fl and a is None:
-                a = c
-            if not fl and a is not None:
-                V.memset(T.mask[GP * i:GP * (i + 1), a:c], 1.0).then_inc(sem.c, 1)
-                nc += 1
-                a = None
-    V.wait_ge(sem.c, nc)
-    TE.wait_ge(sem.c, nc)
-    for s, n in xwaits:
+        V.memset(T.sel[GP * i:GP * (i + 1), i * P:(i + 1) * P], 1.0).then_inc(sem.se, 1)
+
+
+def _table(g, T, route, TR):
+    V, A, sem = g.vector, g.scalar, T.sem
+    V.memset(T.tb[:, :], 0.0).then_inc(sem.c0, 1)
+    V.memset(T.on[:, :], 1.0).then_inc(sem.c0, 1)
+    V.wait_ge(sem.c0, 2)
+    A.wait_ge(sem.c0, 2)
+    done = []
+    for p, r in enumerate(TR):
+        runs = []
+        for i in range(K):
+            for t in range(TOK):
+                assert route[r][t][i] in (i, i + 1)
+            flags = [route[r][t][i] == i for t in range(TOK)] + [False]
+            a = None
+            for c, fl in enumerate(flags):
+                if fl and a is None:
+                    a = c
+                if not fl and a is not None:
+                    runs.append((i, a, c))
+                    a = None
+        nv = na = 0
+        for k, (i, a, c) in enumerate(runs):
+            out = T.tb[GP * i:GP * (i + 1), p * TOK + a:p * TOK + c]
+            if k % 2 == 0:
+                V.memset(out, 1.0).then_inc(sem["t%d" % p], 1)
+                nv += 1
+            else:
+                A.activation(out=out, in_=T.on[GP * i:GP * (i + 1), 0:c - a],
+                             func=ActivationFunctionType.Copy).then_inc(sem["u%d" % p], 1)
+                na += 1
+        done.append([(sem["t%d" % p], nv), (sem["u%d" % p], na)])
+    return done
+
+
+def _gates_split(g, T, gcols, waits):
+    V, sem = g.vector, T.sem
+    nb = len(gcols)
+    W = nb * TOK
+    for s, n in waits:
         V.wait_ge(s, n)
+    for b, (lo, hi) in enumerate(gcols):
+        V.tensor_tensor(out=T.pm[:, b * TOK:(b + 1) * TOK], in0=T.xl[:, lo:hi], in1=T.tb[:, b * TOK:(b + 1) * TOK],
+                        op=AluOpType.mult).then_inc(sem.pm, 1)
+    V.wait_ge(sem.pm, nb)
+    for b, (lo, hi) in enumerate(gcols):
+        V.tensor_tensor(out=T.pm[:, W + b * TOK:W + (b + 1) * TOK], in0=T.xl[:, lo:hi],
+                        in1=T.pm[:, b * TOK:(b + 1) * TOK], op=AluOpType.subtract).then_inc(sem.pm, 1)
+
+
+def _gates_spread(g, T, nb, ER):
+    TE, sem = g.tensor, T.sem
+    W = nb * TOK
+    TE.wait_ge(sem.se, K)
+    TE.wait_ge(sem.pm, 2 * nb)
+    ng = 0
+    for k, e in enumerate(ER):
+        terms = [(i, half) for i, half in ((e, 0), (e - 1, 1)) if 0 <= i < K]
+        for j, (i, half) in enumerate(terms):
+            TE.matmul(out=T.gp[:, k * W:(k + 1) * W], lhsT=T.sel[:, i * P:(i + 1) * P],
+                      rhs=T.pm[:, half * W:(half + 1) * W], start=(j == 0),
+                      stop=(j == len(terms) - 1)).then_inc(sem.gp, 1)
+            ng += 1
+    return ng
+
+
+def _gates_copy(g, T, nb, ER, ng):
+    V, sem = g.vector, T.sem
+    n = len(ER) * nb * TOK
+    V.wait_ge(sem.gp, ng)
+    V.tensor_copy(out=T.gs[:, 0:n], in_=T.gp[:, 0:n]).then_inc(sem.gs, 1)
+    V.wait_ge(sem.gs, 1)
+
+
+def _ffn_z(g, T, ne, xwaits, wwaits):
+    TE, sem = g.tensor, T.sem
+    for s, n in xwaits:
         TE.wait_ge(s, n)
-    for e in range(ne):
-        for p in range(len(TR)):
-            b = e * NT + p * TOK
-            lo, hi = _gc(p)
-            V.tensor_tensor(out=T.pm[:, b:b + TOK], in0=T.xl[:, lo:hi], in1=T.mask[:, b:b + TOK],
-                            op=AluOpType.mult).then_inc(sem.pm, 1)
-    TE.wait_ge(sem.pm, ne * len(TR))
-    TE.matmul(out=T.gp[:, 0:ne * NT], lhsT=T.ones[:, :], rhs=T.pm[:, 0:ne * NT], start=True, stop=True).then_inc(sem.gp, 1)
-    V.wait_ge(sem.gp, 1)
-    V.tensor_copy(out=T.gs[:, 0:ne * NT], in_=T.gp[:, 0:ne * NT]).then_inc(sem.gs, 1)
     for e in range(ne):
         TE.wait_ge(wwaits[e][0], wwaits[e][1])
         for f in range(FT):
             TE.matmul(out=T["z%d" % e][:, f * NT:(f + 1) * NT], lhsT=T.wb[:, e * WS + f * P:e * WS + (f + 1) * P],
                       rhs=T.xl[:, TOK:TOK + NT], start=True, stop=True).then_inc(sem["z%d" % e], 1)
+
+
+def _ffn_h(g, T, ne):
+    V, sem = g.vector, T.sem
     for e in range(ne):
         V.wait_ge(sem["z%d" % e], FT)
         V.tensor_tensor(out=T.h[:, e * FT * NT:(e + 1) * FT * NT], in0=T["z%d" % e][:, 0:FT * NT], in1=T.zero[:, :],
                         op=AluOpType.max).then_inc(sem["h%d" % e], 1)
+
+
+def _ffn_o(g, T, ne):
+    TE, sem = g.tensor, T.sem
     for e in range(ne):
         TE.wait_ge(sem["h%d" % e], 1)
         for f in range(FT):
@@ -94,17 +159,13 @@ def _site(g, T, route, TR, ER, xwaits, wwaits):
             TE.matmul(out=T["o%d" % e][:, 0:NT], lhsT=T.wb[:, w:w + P],
                       rhs=T.h[:, (e * FT + f) * NT:(e * FT + f + 1) * NT],
                       start=(f == 0), stop=(f == FT - 1)).then_inc(sem["o%d" % e], 1)
-    V.wait_ge(sem.gs, 1)
-    for e in range(ne):
-        V.wait_ge(sem["o%d" % e], FT)
-        V.tensor_tensor(out=T.res[:, e * NT:(e + 1) * NT], in0=T["o%d" % e][:, 0:NT], in1=T.gs[:, e * NT:(e + 1) * NT],
-                        op=AluOpType.mult).then_inc(sem.r, 1)
 
 
 def rank_program(g, core, T, topo):
     cores = list(T.cores)
     route = T.tables["ROUTE"]
     sem = T.sem
+    V = g.vector
     hosts = []
     for c in cores:
         if topo.host(c) not in hosts:
@@ -113,7 +174,7 @@ def rank_program(g, core, T, topo):
     helpers = []
     for s, side in enumerate(sides):
         first = cores[side[0]]
-        near = first if TOKEN_RACK else cores[sides[1 - s][0]]
+        near = cores[sides[1 - s][0]]
         pick = None
         for w in range(NSIM):
             if pick is not None or w in cores or topo.host(w) in hosts:
@@ -134,9 +195,29 @@ def rank_program(g, core, T, topo):
         side, far = sides[s], sides[1 - s]
         nx = sum(len(_bits(topo.mask(cores[r], core))) for r in side)
         ww = [(sem["w%d" % e], len(_bits(topo.mask(cores[far[e]], core)))) for e in range(len(far))]
-        _site(g, T, route, side, far, [(sem.xa, nx)], ww)
+        done = _table(g, T, route, side)
+        _consts(g, T)
+        _gates_split(g, T, [_gc(p) for p in range(len(side))], [w for d in done for w in d] + [(sem.xa, nx)])
+        _ffn_z(g, T, len(far), [(sem.xa, nx)], ww)
+        ng = _gates_spread(g, T, len(side), far)
+        _ffn_h(g, T, len(far))
+        _gates_copy(g, T, len(side), far, ng)
+        _ffn_o(g, T, len(far))
+        for e in range(len(far)):
+            V.wait_ge(sem["o%d" % e], FT)
+            V.tensor_tensor(out=T.res[:, e * NT:(e + 1) * NT], in0=T["o%d" % e][:, 0:NT],
+                            in1=T.gs[:, e * NT:(e + 1) * NT], op=AluOpType.mult).then_inc(sem.r, 1)
+        nloc = 0
+        for p, r in enumerate(side):
+            bits = _bits(topo.mask(core, cores[r]))
+            rid, pid = topo.addr(cores[r], core)
+            for sm, n in done[p]:
+                g.wait_ge(sm, n)
+            g.remote_dma(out_ap=T.tb[:, 0:TOK], in_ap=T.tb[:, p * TOK:(p + 1) * TOK], remote_sem=sem.ta,
+                         local_sem=sem.loc, pid=pid, routing_id=rid, dma_engine_mask=_mk(bits))
+            nloc += len(bits)
         g.wait_ge(sem.r, len(far))
-        trs, nloc = [], 0
+        trs = []
         for p, r in enumerate(side):
             bits = _bits(topo.mask(core, cores[r]))
             n = len(bits) // len(side)
@@ -153,10 +234,10 @@ def rank_program(g, core, T, topo):
     s = [rank in side for side in sides].index(True)
     side = sides[s]
     p = side.index(rank)
-    sib = cores[side[1 - p]]
+    q = 1 - p
+    sib = cores[side[q]]
     hx, hw = helpers[s], helpers[1 - s]
     lo, hi = _gc(p)
-    V = g.vector
     V.memset(T.xl[:, lo:hi], 0.0).then_inc(sem.ms, 1)
     g.sync.dma_start(T.xl[:, TOK + p * TOK:TOK + (p + 1) * TOK], T.x[:, :]).then_inc(sem.xld, 16)
     g.scalar.wait_ge(sem.ms, 1)
@@ -185,22 +266,33 @@ def rank_program(g, core, T, topo):
     nloc += len(on)
 
     V.wait_ge(sem.ms, 1)
-    _site(g, T, route, side, [rank], [(sem.xld, 32), (sem.xa, len(on))], [(sem.w0, 32)])
-
+    _consts(g, T)
+    _ffn_z(g, T, 1, [(sem.xld, 32), (sem.xa, len(on))], [(sem.w0, 32)])
+    _ffn_h(g, T, 1)
+    _ffn_o(g, T, 1)
+    V.wait_ge(sem.o0, FT)
+    V.tensor_copy(out=T.res[:, 0:TOK], in_=T.o0[:, q * TOK:(q + 1) * TOK]).then_inc(sem.r, 1)
     g.wait_ge(sem.r, 1)
-    q = 1 - p
-    g.remote_dma(out_ap=T.sl[:, :], in_ap=T.res[:, q * TOK:(q + 1) * TOK], remote_sem=sem.sa,
+    g.remote_dma(out_ap=T.sl[:, :], in_ap=T.res[:, 0:TOK], remote_sem=sem.sa,
                  local_sem=sem.loc, pid=pid, routing_id=rid, dma_engine_mask=_mk(on))
     nloc += len(on)
     g.wait_ge(sem.loc, nloc)
 
-    V.wait_ge(sem.r, 1)
+    home = [rank, side[q]]
+    _gates_split(g, T, [(lo, hi)], [(sem.xld, 32), (sem.ta, len(_bits(topo.mask(hx, core))))])
+    ng = _gates_spread(g, T, 1, home)
+    _gates_copy(g, T, 1, home, ng)
+    V.tensor_tensor(out=T.a0[:, :], in0=T.o0[:, p * TOK:(p + 1) * TOK], in1=T.gs[:, 0:TOK],
+                    op=AluOpType.mult).then_inc(sem.acc, 1)
+    V.tensor_copy(out=T.gb[:, :], in_=T.gs[:, TOK:2 * TOK]).then_inc(sem.gs, 1)
+    V.wait_ge(sem.gs, 2)
     V.wait_ge(sem.sa, len(on))
-    V.tensor_tensor(out=T.acc[:, :], in0=T.res[:, p * TOK:(p + 1) * TOK], in1=T.sl[:, :],
-                    op=AluOpType.add).then_inc(sem.acc, 1)
-    V.wait_ge(sem.acc, 1)
+    V.tensor_tensor(out=T.a1[:, :], in0=T.sl[:, :], in1=T.gb[:, :], op=AluOpType.mult).then_inc(sem.acc, 1)
+    V.wait_ge(sem.acc, 2)
+    V.tensor_tensor(out=T.a2[:, :], in0=T.a0[:, :], in1=T.a1[:, :], op=AluOpType.add).then_inc(sem.acc, 1)
+    V.wait_ge(sem.acc, 3)
     V.wait_ge(sem.fa, len(_bits(topo.mask(hx, core))) // len(side))
-    V.tensor_tensor(out=T.yb[:, :], in0=T.acc[:, :], in1=T.al[:, :], op=AluOpType.add).then_inc(sem.ybs, 1)
+    V.tensor_tensor(out=T.yb[:, :], in0=T.a2[:, :], in1=T.al[:, :], op=AluOpType.add).then_inc(sem.ybs, 1)
     g.sync.wait_ge(sem.ybs, 1)
     g.sync.dma_start(T.y[:, :], T.yb[:, :]).then_inc(sem.yd, 16)
     g.sync.wait_ge(sem.yd, 16)

from concourse.bass import DstId, RemoteDMATransfer
from concourse.mybir import AluOpType, ActivationFunctionType

P = 128
TOK, K, FT = 32, 3, 2
NSIM = 512
NT = 2 * TOK
WS = 2 * FT * P
GP = 32

SCRATCH = {
    "xl": ("sbuf", [P, 2 * NT], "bfloat16"),
    "wb": ("sbuf", [P, 2 * WS], "bfloat16"),
    "sel": ("sbuf", [P, K * P], "bfloat16"),
    "zero": ("sbuf", [P, FT * NT], "float32"),
    "on": ("sbuf", [P, TOK], "bfloat16"),
    "tb": ("sbuf", [P, NT], "bfloat16"),
    "pm": ("sbuf", [P, 2 * NT], "bfloat16"),
    "gs": ("sbuf", [P, 2 * NT], "float32"),
    "gb": ("sbuf", [P, TOK], "bfloat16"),
    "h": ("sbuf", [P, 2 * FT * NT], "bfloat16"),
    "res": ("sbuf", [P, 2 * NT], "bfloat16"),
    "sl": ("sbuf", [P, TOK], "bfloat16"),
    "al": ("sbuf", [P, TOK], "bfloat16"),
    "a0": ("sbuf", [P, TOK], "float32"),
    "a1": ("sbuf", [P, TOK], "float32"),
    "a2": ("sbuf", [P, TOK], "bfloat16"),
    "yb": ("sbuf", [P, TOK], "bfloat16"),
    "z0": ("psum", [P, 512], "float32"),
    "z1": ("psum", [P, 512], "float32"),
    "o0": ("psum", [P, 512], "float32"),
    "o1": ("psum", [P, 512], "float32"),
    "gp": ("psum", [P, 512], "float32"),
}
SEMAPHORES = ["ms", "xld", "xa", "w0", "w1", "c0", "c1", "t0", "t1", "u0", "u1", "se", "zs", "ta", "pm", "gp", "gs",
              "z0", "z1", "h0", "h1", "o0", "o1", "r", "sa", "fa", "acc", "ybs", "yd", "loc"]


def _bits(m):
    return [b for b in range(m.bit_length()) if (m >> b) & 1]


def _mk(bits):
    return sum(1 << b for b in bits)


def _gc(p):
    return (0, TOK) if p == 0 else (2 * NT - TOK, 2 * NT)


def _consts(g, T):
    V, sem = g.vector, T.sem
    V.memset(T.sel[:, :], 0.0).then_inc(sem.c1, 1)
    V.memset(T.zero[:, :], 0.0).then_inc(sem.zs, 1)
    V.wait_ge(sem.c1, 1)
    V.wait_ge(sem.zs, 1)
    for i in range(K):
        V.memset(T.sel[GP * i:GP * (i + 1), i * P:(i + 1) * P], 1.0).then_inc(sem.se, 1)


def _table(g, T, route, TR):
    V, A, sem = g.vector, g.scalar, T.sem
    V.memset(T.tb[:, :], 0.0).then_inc(sem.c0, 1)
    V.memset(T.on[:, :], 1.0).then_inc(sem.c0, 1)
    V.wait_ge(sem.c0, 2)
    A.wait_ge(sem.c0, 2)
    done = []
    for p, r in enumerate(TR):
        runs = []
        for i in range(K):
            for t in range(TOK):
                assert route[r][t][i] in (i, i + 1)
            flags = [route[r][t][i] == i for t in range(TOK)] + [False]
            a = None
            for c, fl in enumerate(flags):
                if fl and a is None:
                    a = c
                if not fl and a is not None:
                    runs.append((i, a, c))
                    a = None
        nv = na = 0
        for k, (i, a, c) in enumerate(runs):
            out = T.tb[GP * i:GP * (i + 1), p * TOK + a:p * TOK + c]
            if k % 2 == 0:
                V.memset(out, 1.0).then_inc(sem["t%d" % p], 1)
                nv += 1
            else:
                A.activation(out=out, in_=T.on[GP * i:GP * (i + 1), 0:c - a],
                             func=ActivationFunctionType.Copy).then_inc(sem["u%d" % p], 1)
                na += 1
        done.append([(sem["t%d" % p], nv), (sem["u%d" % p], na)])
    return done


def _gates_split(g, T, gcols, waits):
    V, sem = g.vector, T.sem
    nb = len(gcols)
    W = nb * TOK
    for s, n in waits:
        V.wait_ge(s, n)
    for b, (lo, hi) in enumerate(gcols):
        V.tensor_tensor(out=T.pm[:, b * TOK:(b + 1) * TOK], in0=T.xl[:, lo:hi], in1=T.tb[:, b * TOK:(b + 1) * TOK],
                        op=AluOpType.mult).then_inc(sem.pm, 1)
    V.wait_ge(sem.pm, nb)
    for b, (lo, hi) in enumerate(gcols):
        V.tensor_tensor(out=T.pm[:, W + b * TOK:W + (b + 1) * TOK], in0=T.xl[:, lo:hi],
                        in1=T.pm[:, b * TOK:(b + 1) * TOK], op=AluOpType.subtract).then_inc(sem.pm, 1)


def _gates_spread(g, T, nb, ER):
    TE, sem = g.tensor, T.sem
    W = nb * TOK
    TE.wait_ge(sem.se, K)
    TE.wait_ge(sem.pm, 2 * nb)
    ng = 0
    for k, e in enumerate(ER):
        terms = [(i, half) for i, half in ((e, 0), (e - 1, 1)) if 0 <= i < K]
        for j, (i, half) in enumerate(terms):
            TE.matmul(out=T.gp[:, k * W:(k + 1) * W], lhsT=T.sel[:, i * P:(i + 1) * P],
                      rhs=T.pm[:, half * W:(half + 1) * W], start=(j == 0),
                      stop=(j == len(terms) - 1)).then_inc(sem.gp, 1)
            ng += 1
    return ng


def _gates_copy(g, T, nb, ER, ng):
    V, sem = g.vector, T.sem
    n = len(ER) * nb * TOK
    V.wait_ge(sem.gp, ng)
    V.tensor_copy(out=T.gs[:, 0:n], in_=T.gp[:, 0:n]).then_inc(sem.gs, 1)
    V.wait_ge(sem.gs, 1)


def _ffn_z(g, T, ne, xwaits, wwaits):
    TE, sem = g.tensor, T.sem
    for s, n in xwaits:
        TE.wait_ge(s, n)
    for e in range(ne):
        TE.wait_ge(wwaits[e][0], wwaits[e][1])
        for f in range(FT):
            TE.matmul(out=T["z%d" % e][:, f * NT:(f + 1) * NT], lhsT=T.wb[:, e * WS + f * P:e * WS + (f + 1) * P],
                      rhs=T.xl[:, TOK:TOK + NT], start=True, stop=True).then_inc(sem["z%d" % e], 1)


def _ffn_h(g, T, ne):
    V, sem = g.vector, T.sem
    for e in range(ne):
        V.wait_ge(sem["z%d" % e], FT)
        V.tensor_tensor(out=T.h[:, e * FT * NT:(e + 1) * FT * NT], in0=T["z%d" % e][:, 0:FT * NT], in1=T.zero[:, :],
                        op=AluOpType.max).then_inc(sem["h%d" % e], 1)


def _ffn_o(g, T, ne):
    TE, sem = g.tensor, T.sem
    for e in range(ne):
        TE.wait_ge(sem["h%d" % e], 1)
        for f in range(FT):
            w = e * WS + FT * P + f * P
            TE.matmul(out=T["o%d" % e][:, 0:NT], lhsT=T.wb[:, w:w + P],
                      rhs=T.h[:, (e * FT + f) * NT:(e * FT + f + 1) * NT],
                      start=(f == 0), stop=(f == FT - 1)).then_inc(sem["o%d" % e], 1)


def rank_program(g, core, T, topo):
    cores = list(T.cores)
    route = T.tables["ROUTE"]
    sem = T.sem
    V = g.vector
    hosts = []
    for c in cores:
        if topo.host(c) not in hosts:
            hosts.append(topo.host(c))
    sides = [[r for r in range(len(cores)) if topo.host(cores[r]) == h] for h in hosts]
    helpers = []
    for s, side in enumerate(sides):
        first = cores[side[0]]
        near = cores[sides[1 - s][0]]
        pick = None
        for w in range(NSIM):
            if pick is not None or w in cores or topo.host(w) in hosts:
                continue
            if topo.chip(w) != topo.chip(first) or topo.die(w) != topo.die(first):
                continue
            if topo.rack(topo.host(w)) != topo.rack(topo.host(near)):
                continue
            if all(topo.may_write(c, w) for c in cores) and all(topo.may_write(w, cores[r]) for r in side):
                pick = w
        helpers.append(pick)

    rank = T.rank_of(core)
    if rank is None:
        if core not in helpers:
            return
        s = helpers.index(core)
        side, far = sides[s], sides[1 - s]
        nx = sum(len(_bits(topo.mask(cores[r], core))) for r in side)
        ww = [(sem["w%d" % e], len(_bits(topo.mask(cores[far[e]], core)))) for e in range(len(far))]
        done = _table(g, T, route, side)
        _consts(g, T)
        _gates_split(g, T, [_gc(p) for p in range(len(side))], [w for d in done for w in d] + [(sem.xa, nx)])
        _ffn_z(g, T, len(far), [(sem.xa, nx)], ww)
        ng = _gates_spread(g, T, len(side), far)
        _ffn_h(g, T, len(far))
        _gates_copy(g, T, len(side), far, ng)
        _ffn_o(g, T, len(far))
        for e in range(len(far)):
            V.wait_ge(sem["o%d" % e], FT)
            V.tensor_tensor(out=T.res[:, e * NT:(e + 1) * NT], in0=T["o%d" % e][:, 0:NT],
                            in1=T.gs[:, e * NT:(e + 1) * NT], op=AluOpType.mult).then_inc(sem.r, 1)
        nloc = 0
        for p, r in enumerate(side):
            bits = _bits(topo.mask(core, cores[r]))
            rid, pid = topo.addr(cores[r], core)
            for sm, n in done[p]:
                g.wait_ge(sm, n)
            g.remote_dma(out_ap=T.tb[:, 0:TOK], in_ap=T.tb[:, p * TOK:(p + 1) * TOK], remote_sem=sem.ta,
                         local_sem=sem.loc, pid=pid, routing_id=rid, dma_engine_mask=_mk(bits))
            nloc += len(bits)
        g.wait_ge(sem.r, len(far))
        trs = []
        for p, r in enumerate(side):
            bits = _bits(topo.mask(core, cores[r]))
            n = len(bits) // len(side)
            rid, pid = topo.addr(cores[r], core)
            trs.append(RemoteDMATransfer(dst_ids=[DstId(rid=rid, pnc=pid)], dma_engine_mask=_mk(bits[p * n:(p + 1) * n]),
                                         remote_sem=sem.fa,
                                         srcs=[T.res[:, e * NT + p * TOK:e * NT + (p + 1) * TOK] for e in range(len(far))],
                                         dsts=[T.al[:, :]], alu_op=1))
            nloc += n
        g.remote_dma_fused(trs, local_sem=sem.loc)
        g.wait_ge(sem.loc, nloc)
        return

    s = [rank in side for side in sides].index(True)
    side = sides[s]
    p = side.index(rank)
    q = 1 - p
    sib = cores[side[q]]
    hx, hw = helpers[s], helpers[1 - s]
    lo, hi = _gc(p)
    V.memset(T.xl[:, lo:hi], 0.0).then_inc(sem.ms, 1)
    g.sync.dma_start(T.xl[:, TOK + p * TOK:TOK + (p + 1) * TOK], T.x[:, :]).then_inc(sem.xld, 16)
    g.scalar.wait_ge(sem.ms, 1)
    g.scalar.dma_start(T.xl[0:GP * (K - 1) + 1:GP, lo:hi], T.gate[:, :]).then_inc(sem.xld, 16)
    g.sync.dma_start(T.wb[:, 0:FT * P], T.w1[:, :]).then_inc(sem.w0, 16)
    g.scalar.dma_start(T.wb[:, FT * P:WS], T.w2[:, :]).then_inc(sem.w0, 16)

    off = _bits(topo.mask(core, hx))
    offw = _bits(topo.mask(core, hw))
    on = [b for b in _bits(topo.mask(core, sib)) if b not in off and b not in offw]
    nloc = 0
    g.wait_ge(sem.ms, 1)
    g.wait_ge(sem.xld, 32)
    rid, pid = topo.addr(hx, core)
    g.remote_dma(out_ap=T.xl[:, p * NT:(p + 1) * NT], in_ap=T.xl[:, p * NT:(p + 1) * NT], remote_sem=sem.xa,
                 local_sem=sem.loc, pid=pid, routing_id=rid, dma_engine_mask=_mk(off))
    nloc += len(off)
    g.wait_ge(sem.w0, 32)
    rid, pid = topo.addr(hw, core)
    g.remote_dma(out_ap=T.wb[:, p * WS:(p + 1) * WS], in_ap=T.wb[:, 0:WS], remote_sem=sem["w%d" % p],
                 local_sem=sem.loc, pid=pid, routing_id=rid, dma_engine_mask=_mk(offw))
    nloc += len(offw)
    rid, pid = topo.addr(sib, core)
    g.remote_dma(out_ap=T.xl[:, p * NT:(p + 1) * NT], in_ap=T.xl[:, p * NT:(p + 1) * NT], remote_sem=sem.xa,
                 local_sem=sem.loc, pid=pid, routing_id=rid, dma_engine_mask=_mk(on))
    nloc += len(on)

    V.wait_ge(sem.ms, 1)
    _consts(g, T)
    _ffn_z(g, T, 1, [(sem.xld, 32), (sem.xa, len(on))], [(sem.w0, 32)])
    _ffn_h(g, T, 1)
    _ffn_o(g, T, 1)
    V.wait_ge(sem.o0, FT)
    V.tensor_copy(out=T.res[:, 0:TOK], in_=T.o0[:, q * TOK:(q + 1) * TOK]).then_inc(sem.r, 1)
    g.wait_ge(sem.r, 1)
    g.remote_dma(out_ap=T.sl[:, :], in_ap=T.res[:, 0:TOK], remote_sem=sem.sa,
                 local_sem=sem.loc, pid=pid, routing_id=rid, dma_engine_mask=_mk(on))
    nloc += len(on)
    g.wait_ge(sem.loc, nloc)

    home = [rank, side[q]]
    _gates_split(g, T, [(lo, hi)], [(sem.xld, 32), (sem.ta, len(_bits(topo.mask(hx, core))))])
    ng = _gates_spread(g, T, 1, home)
    _gates_copy(g, T, 1, home, ng)
    V.tensor_tensor(out=T.a0[:, :], in0=T.o0[:, p * TOK:(p + 1) * TOK], in1=T.gs[:, 0:TOK],
                    op=AluOpType.mult).then_inc(sem.acc, 1)
    V.tensor_copy(out=T.gb[:, :], in_=T.gs[:, TOK:2 * TOK]).then_inc(sem.gs, 1)
    V.wait_ge(sem.gs, 2)
    V.wait_ge(sem.sa, len(on))
    V.tensor_tensor(out=T.a1[:, :], in0=T.sl[:, :], in1=T.gb[:, :], op=AluOpType.mult).then_inc(sem.acc, 1)
    V.wait_ge(sem.acc, 2)
    V.tensor_tensor(out=T.a2[:, :], in0=T.a0[:, :], in1=T.a1[:, :], op=AluOpType.add).then_inc(sem.acc, 1)
    V.wait_ge(sem.acc, 3)
    V.wait_ge(sem.fa, len(_bits(topo.mask(hx, core))) // len(side))
    V.tensor_tensor(out=T.yb[:, :], in0=T.a2[:, :], in1=T.al[:, :], op=AluOpType.add).then_inc(sem.ybs, 1)
    g.sync.wait_ge(sem.ybs, 1)
    g.sync.dma_start(T.y[:, :], T.yb[:, :]).then_inc(sem.yd, 16)
    g.sync.wait_ge(sem.yd, 16)
